import numpy as np
import ml_dtypes


def mxq(x, axis, fmt="e4m3"):
    dtype, down = {"e4m3": (ml_dtypes.float8_e4m3fn, 7), "e5m2": (ml_dtypes.float8_e5m2, 14)}[fmt]
    v = np.moveaxis(np.asarray(x, np.float32).astype(ml_dtypes.bfloat16).astype(np.float64), axis, -1)
    blocks = v.reshape(v.shape[:-1] + (-1, 32))
    amax = np.abs(blocks).max(-1, keepdims=True)
    byte = np.maximum(np.where(amax > 0, np.frexp(amax)[1] - 1 + 127, 0) - down, 1)
    scale = np.exp2(byte - 127.0)
    codes = (blocks / scale).astype(np.float32).astype(dtype).astype(np.float64)
    return np.moveaxis((codes * scale).reshape(v.shape), -1, axis)


WIDE = False


def mx_kscale(k):
    if not WIDE:
        return np.ones(k)
    levels = np.array([10, -10, 5, -5, 0])
    if k % 512:
        return np.exp2(np.random.permutation(np.resize(levels, k // 32))).repeat(32)
    a = np.empty((k // 512, 16))
    for p in range(k // 512):
        a[p, :8] = np.random.permutation(np.resize(levels, 8))
        for g in range(8):
            far = levels[np.abs(levels - a[p, g]) >= 10]
            a[p, g + 8] = far[np.random.randint(len(far))]
    return np.exp2(a.ravel()).repeat(32)


def f64(x):
    return np.asarray(x).astype(np.float64)


def striped(idx):
    return np.tile(idx.reshape(-1, 16).T, (8, 1)).astype(np.uint16)


def unstriped(offs):
    return offs[:16].T.reshape(-1).astype(np.int64)


E2M1 = np.array([0.0, 0.5, 1.0, 1.5, 2.0, 3.0, 4.0, 6.0, -0.0, -0.5, -1.0, -1.5, -2.0, -3.0, -4.0, -6.0])


def pack_weight(w, fmt):
    k, n = w.shape
    w = f64(np.asarray(w, np.float32).astype(ml_dtypes.bfloat16)).reshape(k // 32, 32, n)
    amax = np.abs(w).max(1)
    if fmt == "e4m3":
        byte = np.frexp(amax)[1] - 1 + 127 - 7
    else:
        mant, ex = np.frexp(amax / 6.0)
        byte = np.where(mant > 0.5, ex, ex - 1) + 127
    byte = np.clip(np.where(amax > 0, byte, 1), 1, 254)
    scaled = (w * np.exp2(127.0 - byte)[:, None, :]).reshape(k, n).astype(np.float32)
    by_word = np.ascontiguousarray(scaled.reshape(k // 512, 128, 4, n).transpose(0, 1, 3, 2))
    if fmt == "e4m3":
        words = by_word.astype(ml_dtypes.float8_e4m3fn).view(np.uint8)
    else:
        c = by_word.astype(ml_dtypes.float4_e2m1fn).view(np.uint8) & 0xF
        words = (c[..., 0::2] | (c[..., 1::2] << 4)).reshape(k // 512, 128, 2 * n)
    return np.ascontiguousarray(words), np.ascontiguousarray(byte.astype(np.uint8).reshape(k // 512, 16, n))


def unpack_weight(words, scales, fmt):
    g, _, n = scales.shape
    words = np.ascontiguousarray(words).reshape(g, 128, n, -1)
    if fmt == "e4m3":
        vals = words.view(ml_dtypes.float8_e4m3fn).astype(np.float64)
    else:
        nib = np.empty((g, 128, n, 4), np.uint8)
        nib[..., 0::2] = words & 0xF
        nib[..., 1::2] = words >> 4
        vals = E2M1[nib]
    vals = vals * np.repeat(np.exp2(scales.astype(np.float64) - 127.0), 8, axis=1)[..., None]
    return vals.transpose(0, 1, 3, 2).reshape(g * 512, n)


def gelu(v):
    return 0.5 * v * (1.0 + np.tanh(np.sqrt(2.0 / np.pi) * (v + 0.044715 * v**3)))


K, T, S, H, S2, T3, T2, P = 1024, 2048, 512, 1024, 1024, 2048, 1024, 512

def setup_inputs():
    n = np.random.standard_normal
    s = mx_kscale(K)[:, None]
    u = mx_kscale(H)[:, None]
    tab_words, tab_scales = pack_weight(n((K, T)) * s, "e4m3")
    tab2_words, tab2_scales = pack_weight(n((H, T3)) / np.sqrt(H) / u, "e4m3")
    w1_words, w1_scales = pack_weight(1.5 * n((K, H)) / np.sqrt(K) / s, "e2m1")
    return {
        "tab_words": tab_words, "tab_scales": tab_scales,
        "offs": striped(np.random.permutation(T)[:S]),
        "tab2_words": tab2_words, "tab2_scales": tab2_scales,
        "offs2": striped(np.random.permutation(T3)[:S2]),
        "offs3": striped(np.random.permutation(T2)[:S]),
        "pos1": striped(np.random.permutation(T2)[:P]),
        "pos2": striped(np.random.permutation(T2)[:P]),
        "w1_words": w1_words, "w1_scales": w1_scales,
        "wd": (1.5 * n((K, S2)) / np.sqrt(K) / s).astype(np.float32),
        "gain": (np.random.uniform(0.5, 2.0, H) * u[:, 0]).astype(np.float32),
        "page0": (n((H, T2)) * u).astype(np.float32),
        "wgs": np.exp(0.3 * n((128, S))).astype(np.float32),
        "dump": n(S2).astype(np.float32),
    }

def reference(tab_words, tab_scales, offs, tab2_words, tab2_scales, offs2, offs3, pos1, pos2,
              w1_words, w1_scales, wd, gain, page0, wgs, dump):
    v = unpack_weight(tab_words, tab_scales, "e4m3")[:, unstriped(offs)]
    v2 = unpack_weight(tab2_words, tab2_scales, "e4m3")[:, unstriped(offs2)]
    w1 = unpack_weight(w1_words, w1_scales, "e2m1")
    wq = mxq(f64(wd), 0, "e4m3")
    h = f64(gain)[:, None] * np.tanh(w1.T @ v)
    page = f64(page0).copy()
    page[:, unstriped(offs3)] = np.tile(f64(wgs), (H // 128, 1)) * h
    e = v2.T @ mxq(page, 0, "e4m3")
    d = np.tanh(wq.T @ v)
    ramp = e[:, unstriped(pos1)] - e[:, unstriped(pos2)]
    return ramp * d + f64(dump)[:, None]

@@ -1,0 +1,293 @@
+from contextlib import ExitStack
+
+import concourse.mybir as mybir
+
+K, T, S, H, S2, T3, T2 = 1024, 2048, 512, 1024, 1024, 2048, 1024
+FLOPS = 2 * K * H * S + 2 * H * S2 * T2 + 2 * K * S2 * S
+
+F32 = mybir.dt.float32
+BF16 = mybir.dt.bfloat16
+I32 = mybir.dt.int32
+U32 = mybir.dt.uint32
+U16 = mybir.dt.uint16
+U8 = mybir.dt.uint8
+FP8X4 = mybir.dt.float8_e4m3fn_x4
+FP4X4 = mybir.dt.float4_e2m1fn_x4
+ACT = mybir.ActivationFunctionType
+ALU = mybir.AluOpType
+
+P = 128
+PACK = 4
+PASSES = 2
+K_PASS = P * PACK
+BANK = 512
+PIECE = 512
+QUARTER = 256
+
+
+def tile_list_haul_route_scores_kernel(
+    tc, tab_words, tab_scales, offs, tab2_words, tab2_scales, offs2, offs3, pos1, pos2,
+    w1_words, w1_scales, wd, gain, page0, wgs, dump, out,
+):
+    nc = tc.nc
+    with ExitStack() as ctx:
+        lists = ctx.enter_context(tc.tile_pool(name="lists", bufs=1))
+        keep = ctx.enter_context(tc.tile_pool(name="keep", bufs=1))
+        ring = ctx.enter_context(tc.tile_pool(name="ring", bufs=3))
+        psum = ctx.enter_context(tc.psum_pool(name="psum", bufs=1))
+
+        def load_list(src, name):
+            t = lists.tile([P, src.shape[1]], U16, name=name)
+            nc.sync.dma_start(t[:], src)
+            return t
+
+        def load_words(src, pool, name, tag, bufs):
+            t = pool.tile([P, src.shape[1]], U32, name=name, tag=tag, bufs=bufs, align_bytes=64)
+            nc.sync.dma_start(out=t[:].bitcast(I32), in_=src.rearrange("p t i -> p (t i)").bitcast(I32))
+            return t
+
+        tab_s = keep.tile([P, PASSES, T], U8, name="tab_s", align_bytes=64)
+        w1_s = keep.tile([P, PASSES, H], U8, name="w1_s", align_bytes=64)
+        tab2_s = keep.tile([P, T3], U8, name="tab2_s", align_bytes=64)
+        nc.gpsimd.memset(tab_s[:].bitcast(I32), 0)
+        nc.vector.memset(w1_s[:].bitcast(I32), 0)
+        nc.vector.memset(tab2_s[:].bitcast(I32), 0)
+
+        def load_wd(half, a):
+            t = ring.tile([P, PACK, BANK], F32, name="wd_raw", tag="wide", bufs=4, align_bytes=64)
+            nc.sync.dma_start(
+                out=t[:],
+                in_=wd[a * K_PASS : (a + 1) * K_PASS, half * BANK : (half + 1) * BANK].rearrange(
+                    "(p j) m -> p j m", j=PACK
+                ),
+            )
+            return t
+
+        def load_page(k):
+            b, i = divmod(k, PACK)
+            rows = page0[b * K_PASS : (b + 1) * K_PASS, :].rearrange("(p i) n -> p i n", i=PACK)
+            t = ring.tile([P, T2], F32, name="page", tag="rows", bufs=8)
+            nc.sync.dma_start(out=t[:], in_=rows[:, i, :])
+            return t
+
+        offs_t = load_list(offs, "offs_t")
+        tab_w = [load_words(tab_words[0], ring, "tab_w", "wide", 4)]
+        for q in range(4):
+            nc.sync.dma_start(
+                out=tab_s[32 * q : 32 * q + 4].bitcast(I32),
+                in_=tab_scales[:, 4 * q : 4 * q + 4, :].rearrange("a r t -> r a t").bitcast(I32),
+            )
+        w1_w = keep.tile([P, PASSES, 2 * H], U8, name="w1_w", align_bytes=64)
+        nc.sync.dma_start(out=w1_w[:].bitcast(I32), in_=w1_words.rearrange("a p c -> p a c").bitcast(I32))
+        tab_w.append(load_words(tab_words[1], ring, "tab_w", "wide", 4))
+        for q in range(4):
+            nc.sync.dma_start(
+                out=w1_s[32 * q : 32 * q + 4].bitcast(I32),
+                in_=w1_scales[:, 4 * q : 4 * q + 4, :].rearrange("a r t -> r a t").bitcast(I32),
+            )
+        gain_t = keep.tile([P, PASSES, PACK], F32, name="gain_t")
+        nc.sync.dma_start(out=gain_t[:], in_=gain.rearrange("(b p i) -> p b i", b=PASSES, i=PACK))
+
+        wgs_t = keep.tile([P, PACK, S], F32, name="wgs_t")
+        for q in range(4):
+            nc.sync.dma_start(out=wgs_t[32 * q : 32 * q + 32], in_=wgs.rearrange("(p i) j -> p i j", i=PACK))
+        offs3_t = load_list(offs3, "offs3_t")
+        page = [load_page(k) for k in range(PACK)]
+        wd_raw = {(0, a): load_wd(0, a) for a in range(PASSES)}
+        page.extend(load_page(k) for k in range(PACK, 2 * PACK))
+        offs2_t = load_list(offs2, "offs2_t")
+        for q in range(4):
+            nc.sync.dma_start(
+                out=tab2_s[32 * q : 32 * q + 8].bitcast(I32),
+                in_=tab2_scales[:, 4 * q : 4 * q + 4, :].bitcast(I32),
+            )
+        tab2_w = [load_words(tab2_words[a], keep, "tab2_w%d" % a, "tab2_w%d" % a, 1) for a in range(PASSES)]
+        pos1_t = load_list(pos1, "pos1_t")
+        pos2_t = load_list(pos2, "pos2_t")
+        dump_t = keep.tile([P, S2 // P], F32, name="dump_t")
+        with nc.allow_non_contiguous_dma(reason="one offset a partition"):
+            nc.sync.dma_start(out=dump_t[:], in_=dump.rearrange("(t p) -> p t", p=P))
+        for a in range(PASSES):
+            wd_raw[(1, a)] = load_wd(1, a)
+
+        w1_wp = [keep.tile([P, PASSES, 2 * K_PASS], U8, name="w1_wp%d" % b, align_bytes=64) for b in range(PASSES)]
+        w1_sp = [keep.tile([P, PASSES, K_PASS], U8, name="w1_sp%d" % b, align_bytes=64) for b in range(PASSES)]
+
+        def deal_w1(b):
+            nc.vector.tensor_copy(
+                out=w1_wp[b][:].bitcast(U16).rearrange("p a (i m) -> p a i m", i=PACK),
+                in_=w1_w[:].bitcast(U16)[:, :, b * K_PASS : (b + 1) * K_PASS].rearrange("p a (m i) -> p a i m", i=PACK),
+            )
+            nc.vector.tensor_copy(
+                out=w1_sp[b][:].rearrange("p a (i m) -> p a i m", i=PACK),
+                in_=w1_s[:, :, b * K_PASS : (b + 1) * K_PASS].rearrange("p a (m i) -> p a i m", i=PACK),
+            )
+
+        v_w = [keep.tile([P, S], U32, name="v_w%d" % a, align_bytes=64) for a in range(PASSES)]
+        v_s = [keep.tile([P, S], U8, name="v_s%d" % a, align_bytes=64) for a in range(PASSES)]
+        deal_w1(0)
+        for a in range(PASSES):
+            nc.vector.tensor_copy(v_s[a][:], tab_s[:, a, :].indirect(offs_t[:]))
+        for a in range(PASSES):
+            nc.vector.tensor_copy(v_w[a][:], tab_w[a][:].indirect(offs_t[:]))
+        deal_w1(1)
+
+        def interleave(dst, src):
+            nc.scalar.copy(
+                out=dst.rearrange("p (c k) i -> p c i k", k=4),
+                in_=src.rearrange("p i (c k) -> p c i k", k=4),
+            )
+
+        def quantise(grouped, name):
+            codes = keep.tile([P, grouped.shape[1]], U32, name=name + "_w", align_bytes=64)
+            scales = keep.tile([P, grouped.shape[1]], U8, name=name + "_s", align_bytes=64)
+            nc.vector.quantize_mx(
+                out=codes[:].bitcast(FP8X4), scales=scales[:], in_=grouped[:].rearrange("p n i -> p (n i)")
+            )
+            return codes, scales
+
+        page_q = {}
+        wd_q = {}
+        rounded = [ring.tile([P, PACK, T2], BF16, name="rounded", bufs=2) for b in range(PASSES)]
+
+        def replace(k):
+            b, i = divmod(k, PACK)
+            acc = psum.tile([P, BANK], F32, name="acc_t", bufs=3)
+            for a in range(PASSES):
+                nc.tensor.matmul_mx(
+                    out=acc[:],
+                    lhsT=w1_wp[b][:, a, 2 * i * P : 2 * (i + 1) * P].bitcast(FP4X4),
+                    lhsT_scale=w1_sp[b][:, a, i * P : (i + 1) * P],
+                    rhs=v_w[a][:].bitcast(FP8X4),
+                    rhs_scale=v_s[a][:],
+                    start=(a == 0),
+                    stop=(a == PASSES - 1),
+                )
+            factor = ring.tile([P, S], F32, name="factor", bufs=4)
+            nc.scalar.activation(factor[:], wgs_t[:, i, :], ACT.Copy, scale=gain_t[:, b, i : i + 1])
+            th = ring.tile([P, S], F32, name="th", bufs=4)
+            nc.scalar.activation(th[:], acc[:], ACT.Tanh)
+            nc.vector.tensor_tensor(page[k][:].indirect(offs3_t[:]), th[:], factor[:], ALU.mult)
+
+        def round_rows(k):
+            b, i = divmod(k, PACK)
+            nc.scalar.copy(out=rounded[b][:, i, :], in_=page[k][:])
+
+        def quantise_page(b, half):
+            grouped = ring.tile([P, BANK, PACK], BF16, name="grouped", bufs=4, align_bytes=64)
+            interleave(grouped[:], rounded[b][:, :, half * BANK : (half + 1) * BANK])
+            page_q[(b, half)] = quantise(grouped, "page_q%d%d" % (b, half))
+
+        def quantise_wd(quarter, a):
+            half, col = divmod(quarter * QUARTER, BANK)
+            grouped = ring.tile([P, QUARTER, PACK], BF16, name="grouped", bufs=4, align_bytes=64)
+            interleave(grouped[:], wd_raw[(half, a)][:, :, col : col + QUARTER])
+            wd_q[(quarter, a)] = quantise(grouped, "wd_q%d%d" % (quarter, a))
+
+        v2_w = {}
+        v2_s = {}
+
+        def gather_candidates(c):
+            piece = offs2_t[:, c * PIECE // 16 : (c + 1) * PIECE // 16]
+            v2_s[c] = keep.tile([P, PIECE], U8, name="v2_s%d" % c, align_bytes=64)
+            nc.vector.tensor_copy(v2_s[c][:], tab2_s[:].indirect(piece))
+            for a in range(PASSES):
+                v2_w[(c, a)] = keep.tile([P, PIECE], U32, name="v2_w%d%d" % (c, a), align_bytes=64)
+                nc.vector.tensor_copy(v2_w[(c, a)][:], tab2_w[a][:].indirect(piece))
+
+        AHEAD = 3
+        extra = {
+            3: [lambda: quantise_page(0, 0)],
+            4: [lambda: quantise_page(0, 1)],
+            5: [lambda: quantise_wd(0, 0), lambda: quantise_wd(0, 1)],
+            6: [lambda: quantise_wd(1, 0), lambda: quantise_wd(1, 1)],
+        }
+        for k in range(AHEAD):
+            replace(k)
+        for k in range(2 * PACK):
+            round_rows(k)
+            if k + AHEAD < 2 * PACK:
+                replace(k + AHEAD)
+            for f in extra.get(k, []):
+                f()
+        for c in range(S2 // PIECE):
+            gather_candidates(c)
+        for half in range(2):
+            quantise_page(1, half)
+
+        d = {}
+        e = {}
+
+        def front(mt):
+            c, ccol = divmod(mt * P, PIECE)
+            e[mt] = ring.tile([P, T2], F32, name="e", tag="rows", bufs=8)
+            for nh in range(2):
+                acc_e = psum.tile([P, BANK], F32, name="acc_e", bufs=5)
+                for a in range(PASSES):
+                    codes, scales = page_q[(a, nh)]
+                    nc.tensor.matmul_mx(
+                        out=acc_e[:],
+                        lhsT=v2_w[(c, a)][:, ccol : ccol + P].bitcast(FP8X4),
+                        lhsT_scale=v2_s[c][4 * a : P, ccol : ccol + P],
+                        rhs=codes[:].bitcast(FP8X4),
+                        rhs_scale=scales[:],
+                        start=(a == 0),
+                        stop=(a == PASSES - 1),
+                    )
+                nc.scalar.copy(out=e[mt][:, nh * BANK : (nh + 1) * BANK], in_=acc_e[:])
+
+        def factor_d(mt):
+            quarter, col = divmod(mt * P, QUARTER)
+            acc = psum.tile([P, BANK], F32, name="acc_t", bufs=3)
+            for a in range(PASSES):
+                codes, scales = wd_q[(quarter, a)]
+                nc.tensor.matmul_mx(
+                    out=acc[:],
+                    lhsT=codes[:, col : col + P].bitcast(FP8X4),
+                    lhsT_scale=scales[:, col : col + P],
+                    rhs=v_w[a][:].bitcast(FP8X4),
+                    rhs_scale=v_s[a][:],
+                    start=(a == 0),
+                    stop=(a == PASSES - 1),
+                )
+            d[mt] = ring.tile([P, S], F32, name="d", tag="th", bufs=4)
+            nc.scalar.activation(d[mt][:], acc[:], ACT.Tanh)
+
+        leave = {}
+        ramp = {}
+        prod = {}
+
+        def pick_exit(mt):
+            leave[mt] = ring.tile([P, S], F32, name="leave", bufs=2)
+            nc.vector.tensor_copy(leave[mt][:], e[mt][:].indirect(pos2_t[:]))
+
+        def pick_entry(mt):
+            ramp[mt] = ring.tile([P, S], F32, name="ramp", tag="pair", bufs=3)
+            nc.vector.tensor_tensor(ramp[mt][:], e[mt][:].indirect(pos1_t[:]), leave[mt][:], ALU.subtract)
+
+        def multiply(mt):
+            prod[mt] = ring.tile([P, S], F32, name="prod", tag="pair", bufs=3)
+            nc.vector.tensor_tensor(prod[mt][:], ramp[mt][:], d[mt][:], ALU.mult)
+
+        def finish(mt):
+            res = ring.tile([P, S], F32, name="res", tag="factor", bufs=4)
+            nc.scalar.activation(res[:], prod[mt][:], ACT.Identity, bias=dump_t[:, mt : mt + 1])
+            nc.sync.dma_start(out=out[mt * P : (mt + 1) * P, :], in_=res[:])
+
+        tiles = S2 // P
+        front(0)
+        pick_exit(0)
+        pick_entry(0)
+        for mt in range(tiles):
+            if mt + 1 < tiles:
+                front(mt + 1)
+                pick_exit(mt + 1)
+            factor_d(mt)
+            multiply(mt)
+            if mt > 0:
+                finish(mt - 1)
+            if mt + 1 < tiles:
+                pick_entry(mt + 1)
+            if mt < 4:
+                quantise_wd(2 + mt // PASSES, mt % PASSES)
+        finish(tiles - 1)

@@ -49,12 +49,13 @@ def tile_list_haul_route_scores_kernel(
         tab_s = keep.tile([P, PASSES, T], U8, name="tab_s", align_bytes=64)
         w1_s = keep.tile([P, PASSES, H], U8, name="w1_s", align_bytes=64)
         tab2_s = keep.tile([P, T3], U8, name="tab2_s", align_bytes=64)
-        nc.gpsimd.memset(tab_s[:].bitcast(I32), 0)
+        nc.gpsimd.memset(tab_s[:, 0, :].bitcast(I32), 0)
+        nc.vector.memset(tab_s[:, 1, :].bitcast(I32), 0)
         nc.vector.memset(w1_s[:].bitcast(I32), 0)
         nc.vector.memset(tab2_s[:].bitcast(I32), 0)
 
         def load_wd(half, a):
-            t = ring.tile([P, PACK, BANK], F32, name="wd_raw", tag="wide", bufs=4, align_bytes=64)
+            t = ring.tile([P, PACK, BANK], F32, name="wd_raw", tag="wide", bufs=2, align_bytes=64)
             nc.sync.dma_start(
                 out=t[:],
                 in_=wd[a * K_PASS : (a + 1) * K_PASS, half * BANK : (half + 1) * BANK].rearrange(
@@ -70,8 +71,11 @@ def tile_list_haul_route_scores_kernel(
             nc.sync.dma_start(out=t[:], in_=rows[:, i, :])
             return t
 
+        offs3_t = load_list(offs3, "offs3_t")
+        offs2_t = load_list(offs2, "offs2_t")
+        pos1_t = load_list(pos1, "pos1_t")
         offs_t = load_list(offs, "offs_t")
-        tab_w = [load_words(tab_words[0], ring, "tab_w", "wide", 4)]
+        tab_w = [load_words(tab_words[0], ring, "tab_w", "wide", 2)]
         for q in range(4):
             nc.sync.dma_start(
                 out=tab_s[32 * q : 32 * q + 4].bitcast(I32),
@@ -79,7 +83,7 @@ def tile_list_haul_route_scores_kernel(
             )
         w1_w = keep.tile([P, PASSES, 2 * H], U8, name="w1_w", align_bytes=64)
         nc.sync.dma_start(out=w1_w[:].bitcast(I32), in_=w1_words.rearrange("a p c -> p a c").bitcast(I32))
-        tab_w.append(load_words(tab_words[1], ring, "tab_w", "wide", 4))
+        tab_w.append(load_words(tab_words[1], ring, "tab_w", "wide", 2))
         for q in range(4):
             nc.sync.dma_start(
                 out=w1_s[32 * q : 32 * q + 4].bitcast(I32),
@@ -88,36 +92,30 @@ def tile_list_haul_route_scores_kernel(
         gain_t = keep.tile([P, PASSES, PACK], F32, name="gain_t")
         nc.sync.dma_start(out=gain_t[:], in_=gain.rearrange("(b p i) -> p b i", b=PASSES, i=PACK))
 
-        wgs_t = keep.tile([P, PACK, S], F32, name="wgs_t")
+        wgs_t = ring.tile([P, PACK, S], F32, name="wgs_t", tag="first", bufs=1, align_bytes=64)
         for q in range(4):
             nc.sync.dma_start(out=wgs_t[32 * q : 32 * q + 32], in_=wgs.rearrange("(p i) j -> p i j", i=PACK))
-        offs3_t = load_list(offs3, "offs3_t")
-        page = [load_page(k) for k in range(PACK)]
-        wd_raw = {(0, a): load_wd(0, a) for a in range(PASSES)}
-        page.extend(load_page(k) for k in range(PACK, 2 * PACK))
-        offs2_t = load_list(offs2, "offs2_t")
+        page = [load_page(k) for k in range(2 * PACK)]
         for q in range(4):
             nc.sync.dma_start(
                 out=tab2_s[32 * q : 32 * q + 8].bitcast(I32),
                 in_=tab2_scales[:, 4 * q : 4 * q + 4, :].bitcast(I32),
             )
-        tab2_w = [load_words(tab2_words[a], keep, "tab2_w%d" % a, "tab2_w%d" % a, 1) for a in range(PASSES)]
-        pos1_t = load_list(pos1, "pos1_t")
         pos2_t = load_list(pos2, "pos2_t")
         dump_t = keep.tile([P, S2 // P], F32, name="dump_t")
         with nc.allow_non_contiguous_dma(reason="one offset a partition"):
             nc.sync.dma_start(out=dump_t[:], in_=dump.rearrange("(t p) -> p t", p=P))
-        for a in range(PASSES):
-            wd_raw[(1, a)] = load_wd(1, a)
 
         w1_wp = [keep.tile([P, PASSES, 2 * K_PASS], U8, name="w1_wp%d" % b, align_bytes=64) for b in range(PASSES)]
         w1_sp = [keep.tile([P, PASSES, K_PASS], U8, name="w1_sp%d" % b, align_bytes=64) for b in range(PASSES)]
 
-        def deal_w1(b):
+        def deal_w1_words(b):
             nc.vector.tensor_copy(
                 out=w1_wp[b][:].bitcast(U16).rearrange("p a (i m) -> p a i m", i=PACK),
                 in_=w1_w[:].bitcast(U16)[:, :, b * K_PASS : (b + 1) * K_PASS].rearrange("p a (m i) -> p a i m", i=PACK),
             )
+
+        def deal_w1_scales(b):
             nc.vector.tensor_copy(
                 out=w1_sp[b][:].rearrange("p a (i m) -> p a i m", i=PACK),
                 in_=w1_s[:, :, b * K_PASS : (b + 1) * K_PASS].rearrange("p a (m i) -> p a i m", i=PACK),
@@ -125,12 +123,15 @@ def tile_list_haul_route_scores_kernel(
 
         v_w = [keep.tile([P, S], U32, name="v_w%d" % a, align_bytes=64) for a in range(PASSES)]
         v_s = [keep.tile([P, S], U8, name="v_s%d" % a, align_bytes=64) for a in range(PASSES)]
-        deal_w1(0)
+        nc.vector.tensor_copy(v_w[0][:], tab_w[0][:].indirect(offs_t[:]))
         for a in range(PASSES):
             nc.vector.tensor_copy(v_s[a][:], tab_s[:, a, :].indirect(offs_t[:]))
-        for a in range(PASSES):
-            nc.vector.tensor_copy(v_w[a][:], tab_w[a][:].indirect(offs_t[:]))
-        deal_w1(1)
+        deal_w1_words(0)
+        nc.vector.tensor_copy(v_w[1][:], tab_w[1][:].indirect(offs_t[:]))
+        deal_w1_scales(0)
+        deal_w1_words(1)
+        deal_w1_scales(1)
+        wd_raw = {(0, a): load_wd(0, a) for a in range(PASSES)}
 
         def interleave(dst, src):
             nc.scalar.copy(
@@ -148,7 +149,9 @@ def tile_list_haul_route_scores_kernel(
 
         page_q = {}
         wd_q = {}
-        rounded = [ring.tile([P, PACK, T2], BF16, name="rounded", bufs=2) for b in range(PASSES)]
+        rounded = [
+            ring.tile([P, PACK, T2], BF16, name="rounded", tag=tag, bufs=1, align_bytes=64) for tag in ("second", "third")
+        ]
 
         def replace(k):
             b, i = divmod(k, PACK)
@@ -165,7 +168,8 @@ def tile_list_haul_route_scores_kernel(
                 )
             factor = ring.tile([P, S], F32, name="factor", bufs=4)
             nc.scalar.activation(factor[:], wgs_t[:, i, :], ACT.Copy, scale=gain_t[:, b, i : i + 1])
-            th = ring.tile([P, S], F32, name="th", bufs=4)
+            last = k == 2 * PACK - 1
+            th = ring.tile([P, S], F32, name="th", tag="th_last" if last else "th", bufs=1 if last else 4, align_bytes=64)
             nc.scalar.activation(th[:], acc[:], ACT.Tanh)
             nc.vector.tensor_tensor(page[k][:].indirect(offs3_t[:]), th[:], factor[:], ALU.mult)
 
@@ -174,7 +178,7 @@ def tile_list_haul_route_scores_kernel(
             nc.scalar.copy(out=rounded[b][:, i, :], in_=page[k][:])
 
         def quantise_page(b, half):
-            grouped = ring.tile([P, BANK, PACK], BF16, name="grouped", bufs=4, align_bytes=64)
+            grouped = ring.tile([P, BANK, PACK], BF16, name="page_grouped", tag="half%d" % half, bufs=1, align_bytes=64)
             interleave(grouped[:], rounded[b][:, :, half * BANK : (half + 1) * BANK])
             page_q[(b, half)] = quantise(grouped, "page_q%d%d" % (b, half))
 
@@ -185,35 +189,37 @@ def tile_list_haul_route_scores_kernel(
             wd_q[(quarter, a)] = quantise(grouped, "wd_q%d%d" % (quarter, a))
 
         v2_w = {}
-        v2_s = {}
+        tab2_w = {}
 
-        def gather_candidates(c):
+        def gather_words(c, a, tag):
             piece = offs2_t[:, c * PIECE // 16 : (c + 1) * PIECE // 16]
-            v2_s[c] = keep.tile([P, PIECE], U8, name="v2_s%d" % c, align_bytes=64)
-            nc.vector.tensor_copy(v2_s[c][:], tab2_s[:].indirect(piece))
-            for a in range(PASSES):
-                v2_w[(c, a)] = keep.tile([P, PIECE], U32, name="v2_w%d%d" % (c, a), align_bytes=64)
-                nc.vector.tensor_copy(v2_w[(c, a)][:], tab2_w[a][:].indirect(piece))
+            v2_w[(c, a)] = ring.tile([P, PIECE], U32, name="v2_w", tag=tag, bufs=1, align_bytes=64)
+            nc.vector.tensor_copy(v2_w[(c, a)][:], tab2_w[a][:].indirect(piece))
 
         AHEAD = 3
-        extra = {
-            3: [lambda: quantise_page(0, 0)],
-            4: [lambda: quantise_page(0, 1)],
-            5: [lambda: quantise_wd(0, 0), lambda: quantise_wd(0, 1)],
-            6: [lambda: quantise_wd(1, 0), lambda: quantise_wd(1, 1)],
-        }
         for k in range(AHEAD):
             replace(k)
         for k in range(2 * PACK):
             round_rows(k)
             if k + AHEAD < 2 * PACK:
                 replace(k + AHEAD)
-            for f in extra.get(k, []):
-                f()
-        for c in range(S2 // PIECE):
-            gather_candidates(c)
+            if k == 3:
+                quantise_page(0, 0)
+            if k == 4:
+                tab2_w[0] = load_words(tab2_words[0], ring, "tab2_w", "first", 1)
+                quantise_page(0, 1)
+                tab2_w[1] = load_words(tab2_words[1], ring, "tab2_w", "second", 1)
+            if k == 5:
+                quantise_wd(0, 0)
+                quantise_wd(0, 1)
+        v2_s = ring.tile([P, S2], U8, name="v2_s", tag="th_last", bufs=1, align_bytes=64)
+        nc.vector.tensor_copy(v2_s[:], tab2_s[:].indirect(offs2_t[:]))
+        for a in range(PASSES):
+            gather_words(0, a, "v2_w%d" % a)
         for half in range(2):
             quantise_page(1, half)
+            gather_words(1, half, "half%d" % half)
+        quantise_wd(1, 0)
 
         d = {}
         e = {}
@@ -228,7 +234,7 @@ def tile_list_haul_route_scores_kernel(
                     nc.tensor.matmul_mx(
                         out=acc_e[:],
                         lhsT=v2_w[(c, a)][:, ccol : ccol + P].bitcast(FP8X4),
-                        lhsT_scale=v2_s[c][4 * a : P, ccol : ccol + P],
+                        lhsT_scale=v2_s[4 * a : P, mt * P : (mt + 1) * P],
                         rhs=codes[:].bitcast(FP8X4),
                         rhs_scale=scales[:],
                         start=(a == 0),
@@ -250,7 +256,7 @@ def tile_list_haul_route_scores_kernel(
                     start=(a == 0),
                     stop=(a == PASSES - 1),
                 )
-            d[mt] = ring.tile([P, S], F32, name="d", tag="th", bufs=4)
+            d[mt] = ring.tile([P, S], F32, name="d", tag="th", bufs=4, align_bytes=64)
             nc.scalar.activation(d[mt][:], acc[:], ACT.Tanh)
 
         leave = {}
@@ -261,21 +267,33 @@ def tile_list_haul_route_scores_kernel(
             leave[mt] = ring.tile([P, S], F32, name="leave", bufs=2)
             nc.vector.tensor_copy(leave[mt][:], e[mt][:].indirect(pos2_t[:]))
 
+        def parts(mt):
+            n = 2 if mt + 1 == tiles else 1
+            return [(j * S // n, (j + 1) * S // n) for j in range(n)]
+
         def pick_entry(mt):
             ramp[mt] = ring.tile([P, S], F32, name="ramp", tag="pair", bufs=3)
-            nc.vector.tensor_tensor(ramp[mt][:], e[mt][:].indirect(pos1_t[:]), leave[mt][:], ALU.subtract)
+            for lo, hi in parts(mt):
+                nc.vector.tensor_tensor(
+                    ramp[mt][:, lo:hi], e[mt][:].indirect(pos1_t[:, lo // 16 : hi // 16]), leave[mt][:, lo:hi], ALU.subtract
+                )
 
         def multiply(mt):
             prod[mt] = ring.tile([P, S], F32, name="prod", tag="pair", bufs=3)
-            nc.vector.tensor_tensor(prod[mt][:], ramp[mt][:], d[mt][:], ALU.mult)
+            for lo, hi in parts(mt):
+                nc.vector.tensor_tensor(prod[mt][:, lo:hi], ramp[mt][:, lo:hi], d[mt][:, lo:hi], ALU.mult)
 
         def finish(mt):
             res = ring.tile([P, S], F32, name="res", tag="factor", bufs=4)
-            nc.scalar.activation(res[:], prod[mt][:], ACT.Identity, bias=dump_t[:, mt : mt + 1])
-            nc.sync.dma_start(out=out[mt * P : (mt + 1) * P, :], in_=res[:])
+            for lo, hi in parts(mt):
+                nc.scalar.activation(res[:, lo:hi], prod[mt][:, lo:hi], ACT.Identity, bias=dump_t[:, mt : mt + 1])
+                nc.sync.dma_start(out=out[mt * P : (mt + 1) * P, lo:hi], in_=res[:, lo:hi])
 
         tiles = S2 // P
         front(0)
+        quantise_wd(1, 1)
+        for a in range(PASSES):
+            wd_raw[(1, a)] = load_wd(1, a)
         pick_exit(0)
         pick_entry(0)
         for mt in range(tiles):
@@ -288,6 +306,6 @@ def tile_list_haul_route_scores_kernel(
                 finish(mt - 1)
             if mt + 1 < tiles:
                 pick_entry(mt + 1)
-            if mt < 4:
-                quantise_wd(2 + mt // PASSES, mt % PASSES)
+            if 1 <= mt < 5:
+                quantise_wd(2 + (mt - 1) // PASSES, (mt - 1) % PASSES)
         finish(tiles - 1)

@@ -1,6 +1,7 @@
 from contextlib import ExitStack
 
 import concourse.mybir as mybir
+from concourse.masks import make_identity
 
 K, T, S, H, S2, T3, T2 = 1024, 2048, 512, 1024, 1024, 2048, 1024
 FLOPS = 2 * K * H * S + 2 * H * S2 * T2 + 2 * K * S2 * S
@@ -53,6 +54,8 @@ def tile_list_haul_route_scores_kernel(
         nc.vector.memset(tab_s[:, 1, :].bitcast(I32), 0)
         nc.vector.memset(w1_s[:].bitcast(I32), 0)
         nc.vector.memset(tab2_s[:].bitcast(I32), 0)
+        ident = keep.tile([P, P], F32, name="ident")
+        make_identity(nc, ident[:])
 
         def load_wd(half, a):
             t = ring.tile([P, PACK, BANK], F32, name="wd_raw", tag="wide", bufs=2, align_bytes=64)
@@ -72,39 +75,60 @@ def tile_list_haul_route_scores_kernel(
             return t
 
         offs3_t = load_list(offs3, "offs3_t")
-        offs2_t = load_list(offs2, "offs2_t")
-        pos1_t = load_list(pos1, "pos1_t")
         offs_t = load_list(offs, "offs_t")
-        tab_w = [load_words(tab_words[0], ring, "tab_w", "wide", 2)]
+        gain_t = keep.tile([P, PASSES, PACK], F32, name="gain_t")
+        nc.sync.dma_start(out=gain_t[:], in_=gain.rearrange("(b p i) -> p b i", b=PASSES, i=PACK))
+        wgs_t = keep.tile([P, S], F32, name="wgs_t")
+        nc.sync.dma_start(out=wgs_t[:], in_=wgs)
+        w1_w = keep.tile([P, PASSES, 2 * H], U8, name="w1_w", align_bytes=64)
+        nc.sync.dma_start(out=w1_w[:].bitcast(I32), in_=w1_words.rearrange("a p c -> p a c").bitcast(I32))
         for q in range(4):
             nc.sync.dma_start(
                 out=tab_s[32 * q : 32 * q + 4].bitcast(I32),
                 in_=tab_scales[:, 4 * q : 4 * q + 4, :].rearrange("a r t -> r a t").bitcast(I32),
             )
-        w1_w = keep.tile([P, PASSES, 2 * H], U8, name="w1_w", align_bytes=64)
-        nc.sync.dma_start(out=w1_w[:].bitcast(I32), in_=w1_words.rearrange("a p c -> p a c").bitcast(I32))
-        tab_w.append(load_words(tab_words[1], ring, "tab_w", "wide", 2))
+        tab_w = [load_words(tab_words[a], ring, "tab_w", "wide", 2) for a in range(PASSES)]
         for q in range(4):
             nc.sync.dma_start(
                 out=w1_s[32 * q : 32 * q + 4].bitcast(I32),
                 in_=w1_scales[:, 4 * q : 4 * q + 4, :].rearrange("a r t -> r a t").bitcast(I32),
             )
-        gain_t = keep.tile([P, PASSES, PACK], F32, name="gain_t")
-        nc.sync.dma_start(out=gain_t[:], in_=gain.rearrange("(b p i) -> p b i", b=PASSES, i=PACK))
-
-        wgs_t = ring.tile([P, PACK, S], F32, name="wgs_t", tag="first", bufs=1, align_bytes=64)
-        for q in range(4):
-            nc.sync.dma_start(out=wgs_t[32 * q : 32 * q + 32], in_=wgs.rearrange("(p i) j -> p i j", i=PACK))
         page = [load_page(k) for k in range(2 * PACK)]
         for q in range(4):
             nc.sync.dma_start(
                 out=tab2_s[32 * q : 32 * q + 8].bitcast(I32),
                 in_=tab2_scales[:, 4 * q : 4 * q + 4, :].bitcast(I32),
             )
+        tab2_w = {0: load_words(tab2_words[0], keep, "tab2_w", "first", 1)}
+        offs2_t = load_list(offs2, "offs2_t")
+        pos1_t = load_list(pos1, "pos1_t")
         pos2_t = load_list(pos2, "pos2_t")
         dump_t = keep.tile([P, S2 // P], F32, name="dump_t")
         with nc.allow_non_contiguous_dma(reason="one offset a partition"):
             nc.sync.dma_start(out=dump_t[:], in_=dump.rearrange("(t p) -> p t", p=P))
+
+        turned = psum.tile([P, S // P, P], F32, name="turned", tag="acc_e", bufs=5)
+        for jb in range(S // P):
+            nc.tensor.transpose(turned[:, jb, :], wgs_t[:, jb * P : (jb + 1) * P], ident[:])
+        dealt = []
+        for i in range(PACK):
+            spread = ring.tile([P, S // P, 4, 32], F32, name="spread", bufs=PACK)
+            nc.scalar.copy(
+                out=spread[:],
+                in_=turned[:].rearrange("j b (p i) -> j b i p", i=PACK)[:, :, i : i + 1, :].to_broadcast([P, S // P, 4, 32]),
+            )
+            bank = psum.tile([P, S], F32, name="dealt", tag="acc_e", bufs=5)
+            for jb in range(S // P):
+                nc.tensor.transpose(
+                    bank[:, jb * P : (jb + 1) * P], spread[:, jb].rearrange("j q p -> j (q p)"), ident[:]
+                )
+            dealt.append(bank)
+        factor = []
+        for k in range(2 * PACK):
+            b, i = divmod(k, PACK)
+            t = ring.tile([P, S], F32, name="factor", tag="factor%d" % k, bufs=1, align_bytes=64)
+            nc.scalar.activation(t[:], dealt[i][:], ACT.Copy, scale=gain_t[:, b, i : i + 1])
+            factor.append(t)
 
         w1_wp = [keep.tile([P, PASSES, 2 * K_PASS], U8, name="w1_wp%d" % b, align_bytes=64) for b in range(PASSES)]
         w1_sp = [keep.tile([P, PASSES, K_PASS], U8, name="w1_sp%d" % b, align_bytes=64) for b in range(PASSES)]
@@ -123,11 +147,11 @@ def tile_list_haul_route_scores_kernel(
 
         v_w = [keep.tile([P, S], U32, name="v_w%d" % a, align_bytes=64) for a in range(PASSES)]
         v_s = [keep.tile([P, S], U8, name="v_s%d" % a, align_bytes=64) for a in range(PASSES)]
-        nc.vector.tensor_copy(v_w[0][:], tab_w[0][:].indirect(offs_t[:]))
+        deal_w1_words(0)
         for a in range(PASSES):
             nc.vector.tensor_copy(v_s[a][:], tab_s[:, a, :].indirect(offs_t[:]))
-        deal_w1_words(0)
-        nc.vector.tensor_copy(v_w[1][:], tab_w[1][:].indirect(offs_t[:]))
+        for a in range(PASSES):
+            nc.vector.tensor_copy(v_w[a][:], tab_w[a][:].indirect(offs_t[:]))
         deal_w1_scales(0)
         deal_w1_words(1)
         deal_w1_scales(1)
@@ -166,12 +190,10 @@ def tile_list_haul_route_scores_kernel(
                     start=(a == 0),
                     stop=(a == PASSES - 1),
                 )
-            factor = ring.tile([P, S], F32, name="factor", bufs=4)
-            nc.scalar.activation(factor[:], wgs_t[:, i, :], ACT.Copy, scale=gain_t[:, b, i : i + 1])
             last = k == 2 * PACK - 1
             th = ring.tile([P, S], F32, name="th", tag="th_last" if last else "th", bufs=1 if last else 4, align_bytes=64)
             nc.scalar.activation(th[:], acc[:], ACT.Tanh)
-            nc.vector.tensor_tensor(page[k][:].indirect(offs3_t[:]), th[:], factor[:], ALU.mult)
+            nc.vector.tensor_tensor(page[k][:].indirect(offs3_t[:]), th[:], factor[k][:], ALU.mult)
 
         def round_rows(k):
             b, i = divmod(k, PACK)
@@ -189,7 +211,6 @@ def tile_list_haul_route_scores_kernel(
             wd_q[(quarter, a)] = quantise(grouped, "wd_q%d%d" % (quarter, a))
 
         v2_w = {}
-        tab2_w = {}
 
         def gather_words(c, a, tag):
             piece = offs2_t[:, c * PIECE // 16 : (c + 1) * PIECE // 16]
@@ -206,20 +227,21 @@ def tile_list_haul_route_scores_kernel(
             if k == 3:
                 quantise_page(0, 0)
             if k == 4:
-                tab2_w[0] = load_words(tab2_words[0], ring, "tab2_w", "first", 1)
                 quantise_page(0, 1)
                 tab2_w[1] = load_words(tab2_words[1], ring, "tab2_w", "second", 1)
             if k == 5:
                 quantise_wd(0, 0)
                 quantise_wd(0, 1)
+            if k == 6:
+                quantise_wd(1, 0)
         v2_s = ring.tile([P, S2], U8, name="v2_s", tag="th_last", bufs=1, align_bytes=64)
         nc.vector.tensor_copy(v2_s[:], tab2_s[:].indirect(offs2_t[:]))
         for a in range(PASSES):
-            gather_words(0, a, "v2_w%d" % a)
+            gather_words(0, a, "factor%d" % (2 * PACK - 1 - a))
         for half in range(2):
             quantise_page(1, half)
             gather_words(1, half, "half%d" % half)
-        quantise_wd(1, 0)
+        quantise_wd(1, 1)
 
         d = {}
         e = {}
@@ -281,17 +303,17 @@ def tile_list_haul_route_scores_kernel(
         def multiply(mt):
             prod[mt] = ring.tile([P, S], F32, name="prod", tag="pair", bufs=3)
             for lo, hi in parts(mt):
-                nc.vector.tensor_tensor(prod[mt][:, lo:hi], ramp[mt][:, lo:hi], d[mt][:, lo:hi], ALU.mult)
+                engine = nc.vector if mt + 1 == tiles else nc.gpsimd
+                engine.tensor_tensor(prod[mt][:, lo:hi], ramp[mt][:, lo:hi], d[mt][:, lo:hi], ALU.mult)
 
         def finish(mt):
-            res = ring.tile([P, S], F32, name="res", tag="factor", bufs=4)
+            res = ring.tile([P, S], F32, name="res", bufs=3)
             for lo, hi in parts(mt):
                 nc.scalar.activation(res[:, lo:hi], prod[mt][:, lo:hi], ACT.Identity, bias=dump_t[:, mt : mt + 1])
                 nc.sync.dma_start(out=out[mt * P : (mt + 1) * P, lo:hi], in_=res[:, lo:hi])
 
         tiles = S2 // P
         front(0)
-        quantise_wd(1, 1)
         for a in range(PASSES):
             wd_raw[(1, a)] = load_wd(1, a)
         pick_exit(0)

@@ -80,7 +80,7 @@ def tile_list_haul_route_scores_kernel(
         nc.sync.dma_start(out=gain_t[:], in_=gain.rearrange("(b p i) -> p b i", b=PASSES, i=PACK))
         wgs_t = keep.tile([P, S], F32, name="wgs_t")
         nc.sync.dma_start(out=wgs_t[:], in_=wgs)
-        w1_w = keep.tile([P, PASSES, 2 * H], U8, name="w1_w", align_bytes=64)
+        w1_w = ring.tile([P, PASSES, 2 * H], U8, name="w1_w", tag="first", bufs=1, align_bytes=64)
         nc.sync.dma_start(out=w1_w[:].bitcast(I32), in_=w1_words.rearrange("a p c -> p a c").bitcast(I32))
         for q in range(4):
             nc.sync.dma_start(
@@ -99,13 +99,9 @@ def tile_list_haul_route_scores_kernel(
                 out=tab2_s[32 * q : 32 * q + 8].bitcast(I32),
                 in_=tab2_scales[:, 4 * q : 4 * q + 4, :].bitcast(I32),
             )
-        tab2_w = {0: load_words(tab2_words[0], keep, "tab2_w", "first", 1)}
         offs2_t = load_list(offs2, "offs2_t")
         pos1_t = load_list(pos1, "pos1_t")
         pos2_t = load_list(pos2, "pos2_t")
-        dump_t = keep.tile([P, S2 // P], F32, name="dump_t")
-        with nc.allow_non_contiguous_dma(reason="one offset a partition"):
-            nc.sync.dma_start(out=dump_t[:], in_=dump.rearrange("(t p) -> p t", p=P))
 
         turned = psum.tile([P, S // P, P], F32, name="turned", tag="acc_e", bufs=5)
         for jb in range(S // P):
@@ -150,12 +146,14 @@ def tile_list_haul_route_scores_kernel(
         deal_w1_words(0)
         for a in range(PASSES):
             nc.vector.tensor_copy(v_s[a][:], tab_s[:, a, :].indirect(offs_t[:]))
-        for a in range(PASSES):
-            nc.vector.tensor_copy(v_w[a][:], tab_w[a][:].indirect(offs_t[:]))
+        nc.vector.tensor_copy(v_w[0][:], tab_w[0][:].indirect(offs_t[:]))
+        nc.vector.tensor_copy(v_w[1][:, : S // 2], tab_w[1][:].indirect(offs_t[:, : S // 32]))
         deal_w1_scales(0)
+        nc.vector.tensor_copy(v_w[1][:, S // 2 :], tab_w[1][:].indirect(offs_t[:, S // 32 :]))
         deal_w1_words(1)
         deal_w1_scales(1)
         wd_raw = {(0, a): load_wd(0, a) for a in range(PASSES)}
+        tab2_w = {0: load_words(tab2_words[0], ring, "tab2_w", "first", 1)}
 
         def interleave(dst, src):
             nc.scalar.copy(
@@ -177,23 +175,29 @@ def tile_list_haul_route_scores_kernel(
             ring.tile([P, PACK, T2], BF16, name="rounded", tag=tag, bufs=1, align_bytes=64) for tag in ("second", "third")
         ]
 
+        def halves(split):
+            return [(0, S // 2), (S // 2, S)] if split else [(0, S)]
+
         def replace(k):
             b, i = divmod(k, PACK)
-            acc = psum.tile([P, BANK], F32, name="acc_t", bufs=3)
-            for a in range(PASSES):
-                nc.tensor.matmul_mx(
-                    out=acc[:],
-                    lhsT=w1_wp[b][:, a, 2 * i * P : 2 * (i + 1) * P].bitcast(FP4X4),
-                    lhsT_scale=w1_sp[b][:, a, i * P : (i + 1) * P],
-                    rhs=v_w[a][:].bitcast(FP8X4),
-                    rhs_scale=v_s[a][:],
-                    start=(a == 0),
-                    stop=(a == PASSES - 1),
-                )
             last = k == 2 * PACK - 1
             th = ring.tile([P, S], F32, name="th", tag="th_last" if last else "th", bufs=1 if last else 4, align_bytes=64)
-            nc.scalar.activation(th[:], acc[:], ACT.Tanh)
-            nc.vector.tensor_tensor(page[k][:].indirect(offs3_t[:]), th[:], factor[k][:], ALU.mult)
+            for lo, hi in halves(k == 0):
+                acc = psum.tile([P, hi - lo], F32, name="acc_t", bufs=3)
+                for a in range(PASSES):
+                    nc.tensor.matmul_mx(
+                        out=acc[:],
+                        lhsT=w1_wp[b][:, a, 2 * i * P : 2 * (i + 1) * P].bitcast(FP4X4),
+                        lhsT_scale=w1_sp[b][:, a, i * P : (i + 1) * P],
+                        rhs=v_w[a][:, lo:hi].bitcast(FP8X4),
+                        rhs_scale=v_s[a][:, lo:hi],
+                        start=(a == 0),
+                        stop=(a == PASSES - 1),
+                    )
+                nc.scalar.activation(th[:, lo:hi], acc[:], ACT.Tanh)
+                nc.vector.tensor_tensor(
+                    page[k][:].indirect(offs3_t[:, lo // 16 : hi // 16]), th[:, lo:hi], factor[k][:, lo:hi], ALU.mult
+                )
 
         def round_rows(k):
             b, i = divmod(k, PACK)
@@ -220,20 +224,28 @@ def tile_list_haul_route_scores_kernel(
         AHEAD = 3
         for k in range(AHEAD):
             replace(k)
+        dump_t = ring.tile([P, S2 // P], F32, name="dump_t", tag="factor0", bufs=1, align_bytes=64)
+        with nc.allow_non_contiguous_dma(reason="one offset a partition"):
+            nc.sync.dma_start(out=dump_t[:], in_=dump.rearrange("(t p) -> p t", p=P))
         for k in range(2 * PACK):
             round_rows(k)
             if k + AHEAD < 2 * PACK:
                 replace(k + AHEAD)
+            if k == 2:
+                quantise_wd(0, 0)
+                quantise_wd(1, 0)
+                wd_raw[(1, 0)] = load_wd(1, 0)
             if k == 3:
                 quantise_page(0, 0)
             if k == 4:
                 quantise_page(0, 1)
                 tab2_w[1] = load_words(tab2_words[1], ring, "tab2_w", "second", 1)
             if k == 5:
-                quantise_wd(0, 0)
                 quantise_wd(0, 1)
+                quantise_wd(1, 1)
+                wd_raw[(1, 1)] = load_wd(1, 1)
             if k == 6:
-                quantise_wd(1, 0)
+                quantise_wd(2, 0)
         v2_s = ring.tile([P, S2], U8, name="v2_s", tag="th_last", bufs=1, align_bytes=64)
         nc.vector.tensor_copy(v2_s[:], tab2_s[:].indirect(offs2_t[:]))
         for a in range(PASSES):
@@ -241,7 +253,7 @@ def tile_list_haul_route_scores_kernel(
         for half in range(2):
             quantise_page(1, half)
             gather_words(1, half, "half%d" % half)
-        quantise_wd(1, 1)
+        quantise_wd(2, 1)
 
         d = {}
         e = {}
@@ -287,47 +299,45 @@ def tile_list_haul_route_scores_kernel(
 
         def pick_exit(mt):
             leave[mt] = ring.tile([P, S], F32, name="leave", bufs=2)
-            nc.vector.tensor_copy(leave[mt][:], e[mt][:].indirect(pos2_t[:]))
+            for lo, hi in halves(True):
+                nc.vector.tensor_copy(leave[mt][:, lo:hi], e[mt][:].indirect(pos2_t[:, lo // 16 : hi // 16]))
 
         def parts(mt):
             n = 2 if mt + 1 == tiles else 1
             return [(j * S // n, (j + 1) * S // n) for j in range(n)]
 
         def pick_entry(mt):
-            ramp[mt] = ring.tile([P, S], F32, name="ramp", tag="pair", bufs=3)
-            for lo, hi in parts(mt):
+            ramp[mt] = ring.tile([P, S], F32, name="ramp", bufs=4)
+            for lo, hi in halves(True):
                 nc.vector.tensor_tensor(
                     ramp[mt][:, lo:hi], e[mt][:].indirect(pos1_t[:, lo // 16 : hi // 16]), leave[mt][:, lo:hi], ALU.subtract
                 )
 
         def multiply(mt):
-            prod[mt] = ring.tile([P, S], F32, name="prod", tag="pair", bufs=3)
+            prod[mt] = ring.tile([P, S], F32, name="prod", bufs=4)
             for lo, hi in parts(mt):
                 engine = nc.vector if mt + 1 == tiles else nc.gpsimd
                 engine.tensor_tensor(prod[mt][:, lo:hi], ramp[mt][:, lo:hi], d[mt][:, lo:hi], ALU.mult)
 
         def finish(mt):
-            res = ring.tile([P, S], F32, name="res", bufs=3)
+            res = ring.tile([P, S], F32, name="res", bufs=4)
             for lo, hi in parts(mt):
                 nc.scalar.activation(res[:, lo:hi], prod[mt][:, lo:hi], ACT.Identity, bias=dump_t[:, mt : mt + 1])
                 nc.sync.dma_start(out=out[mt * P : (mt + 1) * P, lo:hi], in_=res[:, lo:hi])
 
         tiles = S2 // P
         front(0)
-        for a in range(PASSES):
-            wd_raw[(1, a)] = load_wd(1, a)
         pick_exit(0)
-        pick_entry(0)
         for mt in range(tiles):
             if mt + 1 < tiles:
                 front(mt + 1)
                 pick_exit(mt + 1)
             factor_d(mt)
+            if mt >= 2:
+                finish(mt - 2)
+            pick_entry(mt)
             multiply(mt)
-            if mt > 0:
-                finish(mt - 1)
-            if mt + 1 < tiles:
-                pick_entry(mt + 1)
-            if 1 <= mt < 5:
-                quantise_wd(2 + (mt - 1) // PASSES, (mt - 1) % PASSES)
+            if mt in (1, 2):
+                quantise_wd(3, mt - 1)
+        finish(tiles - 2)
         finish(tiles - 1)

from contextlib import ExitStack

import concourse.mybir as mybir
from concourse.masks import make_identity

K, T, S, H, S2, T3, T2 = 1024, 2048, 512, 1024, 1024, 2048, 1024
FLOPS = 2 * K * H * S + 2 * H * S2 * T2 + 2 * K * S2 * S

F32 = mybir.dt.float32
BF16 = mybir.dt.bfloat16
I32 = mybir.dt.int32
U32 = mybir.dt.uint32
U16 = mybir.dt.uint16
U8 = mybir.dt.uint8
FP8X4 = mybir.dt.float8_e4m3fn_x4
FP4X4 = mybir.dt.float4_e2m1fn_x4
ACT = mybir.ActivationFunctionType
ALU = mybir.AluOpType

P = 128
PACK = 4
PASSES = 2
K_PASS = P * PACK
BANK = 512
PIECE = 512
QUARTER = 256


def tile_list_haul_route_scores_kernel(
    tc, tab_words, tab_scales, offs, tab2_words, tab2_scales, offs2, offs3, pos1, pos2,
    w1_words, w1_scales, wd, gain, page0, wgs, dump, out,
):
    nc = tc.nc
    with ExitStack() as ctx:
        lists = ctx.enter_context(tc.tile_pool(name="lists", bufs=1))
        keep = ctx.enter_context(tc.tile_pool(name="keep", bufs=1))
        ring = ctx.enter_context(tc.tile_pool(name="ring", bufs=3))
        psum = ctx.enter_context(tc.psum_pool(name="psum", bufs=1))

        def load_list(src, name):
            t = lists.tile([P, src.shape[1]], U16, name=name)
            nc.sync.dma_start(t[:], src)
            return t

        def load_words(src, pool, name, tag, bufs):
            t = pool.tile([P, src.shape[1]], U32, name=name, tag=tag, bufs=bufs, align_bytes=64)
            nc.sync.dma_start(out=t[:].bitcast(I32), in_=src.rearrange("p t i -> p (t i)").bitcast(I32))
            return t

        tab_s = keep.tile([P, PASSES, T], U8, name="tab_s", align_bytes=64)
        w1_s = keep.tile([P, PASSES, H], U8, name="w1_s", align_bytes=64)
        tab2_s = keep.tile([P, T3], U8, name="tab2_s", align_bytes=64)
        nc.gpsimd.memset(tab_s[:, 0, :].bitcast(I32), 0)
        nc.vector.memset(tab_s[:, 1, :].bitcast(I32), 0)
        nc.vector.memset(w1_s[:].bitcast(I32), 0)
        nc.vector.memset(tab2_s[:].bitcast(I32), 0)
        ident = keep.tile([P, P], F32, name="ident")
        make_identity(nc, ident[:])

        def load_wd(half, a):
            t = ring.tile([P, PACK, BANK], F32, name="wd_raw", tag="wide", bufs=2, align_bytes=64)
            nc.sync.dma_start(
                out=t[:],
                in_=wd[a * K_PASS : (a + 1) * K_PASS, half * BANK : (half + 1) * BANK].rearrange(
                    "(p j) m -> p j m", j=PACK
                ),
            )
            return t

        def load_page(k):
            b, i = divmod(k, PACK)
            rows = page0[b * K_PASS : (b + 1) * K_PASS, :].rearrange("(p i) n -> p i n", i=PACK)
            t = ring.tile([P, T2], F32, name="page", tag="rows", bufs=8)
            nc.sync.dma_start(out=t[:], in_=rows[:, i, :])
            return t

        offs3_t = load_list(offs3, "offs3_t")
        offs_t = load_list(offs, "offs_t")
        gain_t = keep.tile([P, PASSES, PACK], F32, name="gain_t")
        nc.sync.dma_start(out=gain_t[:], in_=gain.rearrange("(b p i) -> p b i", b=PASSES, i=PACK))
        wgs_t = keep.tile([P, S], F32, name="wgs_t")
        nc.sync.dma_start(out=wgs_t[:], in_=wgs)
        w1_w = ring.tile([P, PASSES, 2 * H], U8, name="w1_w", tag="first", bufs=1, align_bytes=64)
        nc.sync.dma_start(out=w1_w[:].bitcast(I32), in_=w1_words.rearrange("a p c -> p a c").bitcast(I32))
        for q in range(4):
            nc.sync.dma_start(
                out=tab_s[32 * q : 32 * q + 4].bitcast(I32),
                in_=tab_scales[:, 4 * q : 4 * q + 4, :].rearrange("a r t -> r a t").bitcast(I32),
            )
        tab_w = [load_words(tab_words[a], ring, "tab_w", "wide", 2) for a in range(PASSES)]
        for q in range(4):
            nc.sync.dma_start(
                out=w1_s[32 * q : 32 * q + 4].bitcast(I32),
                in_=w1_scales[:, 4 * q : 4 * q + 4, :].rearrange("a r t -> r a t").bitcast(I32),
            )
        page = [load_page(k) for k in range(2 * PACK)]
        for q in range(4):
            nc.sync.dma_start(
                out=tab2_s[32 * q : 32 * q + 8].bitcast(I32),
                in_=tab2_scales[:, 4 * q : 4 * q + 4, :].bitcast(I32),
            )
        offs2_t = load_list(offs2, "offs2_t")
        pos1_t = load_list(pos1, "pos1_t")
        pos2_t = load_list(pos2, "pos2_t")

        turned = psum.tile([P, S // P, P], F32, name="turned", tag="acc_e", bufs=5)
        for jb in range(S // P):
            nc.tensor.transpose(turned[:, jb, :], wgs_t[:, jb * P : (jb + 1) * P], ident[:])
        dealt = []
        for i in range(PACK):
            spread = ring.tile([P, S // P, 4, 32], F32, name="spread", bufs=PACK)
            nc.scalar.copy(
                out=spread[:],
                in_=turned[:].rearrange("j b (p i) -> j b i p", i=PACK)[:, :, i : i + 1, :].to_broadcast([P, S // P, 4, 32]),
            )
            bank = psum.tile([P, S], F32, name="dealt", tag="acc_e", bufs=5)
            for jb in range(S // P):
                nc.tensor.transpose(
                    bank[:, jb * P : (jb + 1) * P], spread[:, jb].rearrange("j q p -> j (q p)"), ident[:]
                )
            dealt.append(bank)
        factor = []
        for k in range(2 * PACK):
            b, i = divmod(k, PACK)
            t = ring.tile([P, S], F32, name="factor", tag="factor%d" % k, bufs=1, align_bytes=64)
            nc.scalar.activation(t[:], dealt[i][:], ACT.Copy, scale=gain_t[:, b, i : i + 1])
            factor.append(t)

        w1_wp = [keep.tile([P, PASSES, 2 * K_PASS], U8, name="w1_wp%d" % b, align_bytes=64) for b in range(PASSES)]
        w1_sp = [keep.tile([P, PASSES, K_PASS], U8, name="w1_sp%d" % b, align_bytes=64) for b in range(PASSES)]

        def deal_w1_words(b):
            nc.vector.tensor_copy(
                out=w1_wp[b][:].bitcast(U16).rearrange("p a (i m) -> p a i m", i=PACK),
                in_=w1_w[:].bitcast(U16)[:, :, b * K_PASS : (b + 1) * K_PASS].rearrange("p a (m i) -> p a i m", i=PACK),
            )

        def deal_w1_scales(b):
            nc.vector.tensor_copy(
                out=w1_sp[b][:].rearrange("p a (i m) -> p a i m", i=PACK),
                in_=w1_s[:, :, b * K_PASS : (b + 1) * K_PASS].rearrange("p a (m i) -> p a i m", i=PACK),
            )

        v_w = [keep.tile([P, S], U32, name="v_w%d" % a, align_bytes=64) for a in range(PASSES)]
        v_s = [keep.tile([P, S], U8, name="v_s%d" % a, align_bytes=64) for a in range(PASSES)]
        deal_w1_words(0)
        for a in range(PASSES):
            nc.vector.tensor_copy(v_s[a][:], tab_s[:, a, :].indirect(offs_t[:]))
        nc.vector.tensor_copy(v_w[0][:], tab_w[0][:].indirect(offs_t[:]))
        nc.vector.tensor_copy(v_w[1][:, : S // 2], tab_w[1][:].indirect(offs_t[:, : S // 32]))
        deal_w1_scales(0)
        nc.vector.tensor_copy(v_w[1][:, S // 2 :], tab_w[1][:].indirect(offs_t[:, S // 32 :]))
        deal_w1_words(1)
        deal_w1_scales(1)
        wd_raw = {(0, a): load_wd(0, a) for a in range(PASSES)}
        tab2_w = {0: load_words(tab2_words[0], ring, "tab2_w", "first", 1)}

        def interleave(dst, src):
            nc.scalar.copy(
                out=dst.rearrange("p (c k) i -> p c i k", k=4),
                in_=src.rearrange("p i (c k) -> p c i k", k=4),
            )

        def quantise(grouped, name):
            codes = keep.tile([P, grouped.shape[1]], U32, name=name + "_w", align_bytes=64)
            scales = keep.tile([P, grouped.shape[1]], U8, name=name + "_s", align_bytes=64)
            nc.vector.quantize_mx(
                out=codes[:].bitcast(FP8X4), scales=scales[:], in_=grouped[:].rearrange("p n i -> p (n i)")
            )
            return codes, scales

        page_q = {}
        wd_q = {}
        rounded = [
            ring.tile([P, PACK, T2], BF16, name="rounded", tag=tag, bufs=1, align_bytes=64) for tag in ("second", "third")
        ]

        def halves(split):
            return [(0, S // 2), (S // 2, S)] if split else [(0, S)]

        def replace(k):
            b, i = divmod(k, PACK)
            last = k == 2 * PACK - 1
            th = ring.tile([P, S], F32, name="th", tag="th_last" if last else "th", bufs=1 if last else 4, align_bytes=64)
            for lo, hi in halves(k == 0):
                acc = psum.tile([P, hi - lo], F32, name="acc_t", bufs=3)
                for a in range(PASSES):
                    nc.tensor.matmul_mx(
                        out=acc[:],
                        lhsT=w1_wp[b][:, a, 2 * i * P : 2 * (i + 1) * P].bitcast(FP4X4),
                        lhsT_scale=w1_sp[b][:, a, i * P : (i + 1) * P],
                        rhs=v_w[a][:, lo:hi].bitcast(FP8X4),
                        rhs_scale=v_s[a][:, lo:hi],
                        start=(a == 0),
                        stop=(a == PASSES - 1),
                    )
                nc.scalar.activation(th[:, lo:hi], acc[:], ACT.Tanh)
                nc.vector.tensor_tensor(
                    page[k][:].indirect(offs3_t[:, lo // 16 : hi // 16]), th[:, lo:hi], factor[k][:, lo:hi], ALU.mult
                )

        def round_rows(k):
            b, i = divmod(k, PACK)
            nc.scalar.copy(out=rounded[b][:, i, :], in_=page[k][:])

        def quantise_page(b, half):
            grouped = ring.tile([P, BANK, PACK], BF16, name="page_grouped", tag="half%d" % half, bufs=1, align_bytes=64)
            interleave(grouped[:], rounded[b][:, :, half * BANK : (half + 1) * BANK])
            page_q[(b, half)] = quantise(grouped, "page_q%d%d" % (b, half))

        def quantise_wd(quarter, a):
            half, col = divmod(quarter * QUARTER, BANK)
            grouped = ring.tile([P, QUARTER, PACK], BF16, name="grouped", bufs=4, align_bytes=64)
            interleave(grouped[:], wd_raw[(half, a)][:, :, col : col + QUARTER])
            wd_q[(quarter, a)] = quantise(grouped, "wd_q%d%d" % (quarter, a))

        v2_w = {}

        def gather_words(c, a, tag):
            piece = offs2_t[:, c * PIECE // 16 : (c + 1) * PIECE // 16]
            v2_w[(c, a)] = ring.tile([P, PIECE], U32, name="v2_w", tag=tag, bufs=1, align_bytes=64)
            nc.vector.tensor_copy(v2_w[(c, a)][:], tab2_w[a][:].indirect(piece))

        AHEAD = 3
        for k in range(AHEAD):
            replace(k)
        dump_t = ring.tile([P, S2 // P], F32, name="dump_t", tag="factor0", bufs=1, align_bytes=64)
        with nc.allow_non_contiguous_dma(reason="one offset a partition"):
            nc.sync.dma_start(out=dump_t[:], in_=dump.rearrange("(t p) -> p t", p=P))
        for k in range(2 * PACK):
            round_rows(k)
            if k + AHEAD < 2 * PACK:
                replace(k + AHEAD)
            if k == 2:
                quantise_wd(0, 0)
                quantise_wd(1, 0)
                wd_raw[(1, 0)] = load_wd(1, 0)
            if k == 3:
                quantise_page(0, 0)
            if k == 4:
                quantise_page(0, 1)
                tab2_w[1] = load_words(tab2_words[1], ring, "tab2_w", "second", 1)
            if k == 5:
                quantise_wd(0, 1)
                quantise_wd(1, 1)
                wd_raw[(1, 1)] = load_wd(1, 1)
            if k == 6:
                quantise_wd(2, 0)
        v2_s = ring.tile([P, S2], U8, name="v2_s", tag="th_last", bufs=1, align_bytes=64)
        nc.vector.tensor_copy(v2_s[:], tab2_s[:].indirect(offs2_t[:]))
        for a in range(PASSES):
            gather_words(0, a, "factor%d" % (2 * PACK - 1 - a))
        for half in range(2):
            quantise_page(1, half)
            gather_words(1, half, "half%d" % half)
        quantise_wd(2, 1)

        d = {}
        e = {}

        def front(mt):
            c, ccol = divmod(mt * P, PIECE)
            e[mt] = ring.tile([P, T2], F32, name="e", tag="rows", bufs=8)
            for nh in range(2):
                acc_e = psum.tile([P, BANK], F32, name="acc_e", bufs=5)
                for a in range(PASSES):
                    codes, scales = page_q[(a, nh)]
                    nc.tensor.matmul_mx(
                        out=acc_e[:],
                        lhsT=v2_w[(c, a)][:, ccol : ccol + P].bitcast(FP8X4),
                        lhsT_scale=v2_s[4 * a : P, mt * P : (mt + 1) * P],
                        rhs=codes[:].bitcast(FP8X4),
                        rhs_scale=scales[:],
                        start=(a == 0),
                        stop=(a == PASSES - 1),
                    )
                nc.scalar.copy(out=e[mt][:, nh * BANK : (nh + 1) * BANK], in_=acc_e[:])

        def factor_d(mt):
            quarter, col = divmod(mt * P, QUARTER)
            acc = psum.tile([P, BANK], F32, name="acc_t", bufs=3)
            for a in range(PASSES):
                codes, scales = wd_q[(quarter, a)]
                nc.tensor.matmul_mx(
                    out=acc[:],
                    lhsT=codes[:, col : col + P].bitcast(FP8X4),
                    lhsT_scale=scales[:, col : col + P],
                    rhs=v_w[a][:].bitcast(FP8X4),
                    rhs_scale=v_s[a][:],
                    start=(a == 0),
                    stop=(a == PASSES - 1),
                )
            d[mt] = ring.tile([P, S], F32, name="d", tag="th", bufs=4, align_bytes=64)
            nc.scalar.activation(d[mt][:], acc[:], ACT.Tanh)

        leave = {}
        ramp = {}
        prod = {}

        def pick_exit(mt):
            leave[mt] = ring.tile([P, S], F32, name="leave", bufs=2)
            for lo, hi in halves(True):
                nc.vector.tensor_copy(leave[mt][:, lo:hi], e[mt][:].indirect(pos2_t[:, lo // 16 : hi // 16]))

        def parts(mt):
            n = 2 if mt + 1 == tiles else 1
            return [(j * S // n, (j + 1) * S // n) for j in range(n)]

        def pick_entry(mt):
            ramp[mt] = ring.tile([P, S], F32, name="ramp", bufs=4)
            for lo, hi in halves(True):
                nc.vector.tensor_tensor(
                    ramp[mt][:, lo:hi], e[mt][:].indirect(pos1_t[:, lo // 16 : hi // 16]), leave[mt][:, lo:hi], ALU.subtract
                )

        def multiply(mt):
            prod[mt] = ring.tile([P, S], F32, name="prod", bufs=4)
            for lo, hi in parts(mt):
                engine = nc.vector if mt + 1 == tiles else nc.gpsimd
                engine.tensor_tensor(prod[mt][:, lo:hi], ramp[mt][:, lo:hi], d[mt][:, lo:hi], ALU.mult)

        def finish(mt):
            res = ring.tile([P, S], F32, name="res", bufs=4)
            for lo, hi in parts(mt):
                nc.scalar.activation(res[:, lo:hi], prod[mt][:, lo:hi], ACT.Identity, bias=dump_t[:, mt : mt + 1])
                nc.sync.dma_start(out=out[mt * P : (mt + 1) * P, lo:hi], in_=res[:, lo:hi])

        tiles = S2 // P
        front(0)
        pick_exit(0)
        for mt in range(tiles):
            if mt + 1 < tiles:
                front(mt + 1)
                pick_exit(mt + 1)
            factor_d(mt)
            if mt >= 2:
                finish(mt - 2)
            pick_entry(mt)
            multiply(mt)
            if mt in (1, 2):
                quantise_wd(3, mt - 1)
        finish(tiles - 2)
        finish(tiles - 1)
